import numpy as np, ml_dtypes
CORES = [66,74,82,90,194,202,210,218]
N = 8
import mx_ref
BF = ml_dtypes.bfloat16
def gentries(a):
    return np.ascontiguousarray(a.reshape(8, 16, -1).transpose(0, 2, 1)).reshape(8, -1)
def gtable(e):
    e = np.asarray(e); return np.ascontiguousarray(e.reshape(8, -1, 16).transpose(0, 2, 1)).reshape(128, -1).astype(np.int32)
def gcols(t, e):
    v = np.concatenate([t.reshape(8, 16, -1, 4), np.zeros((8, 16, 1, 4), BF)], axis=2)
    return np.ascontiguousarray(np.stack([v[g][:, e[g]] for g in range(8)])).reshape(128, -1)
def gpick(z, e):
    return np.concatenate([z[16 * g:16 * g + 16][:, e[g]] for g in range(8)])
def tile(rs):
    return np.stack(rs, axis=2).reshape(128, -1).astype(BF)
def pick(q, e):
    c = np.concatenate([q[0].reshape(128, -1, 4), np.zeros((128, 1, 4), np.uint8)], axis=1); s = np.concatenate([q[1], np.ones((16, 1), np.uint8)], axis=1)
    return (np.ascontiguousarray(c[:, e].reshape(128, -1)), np.ascontiguousarray(s[:, e]))
def join(*qs):
    return (np.concatenate([q[0] for q in qs], axis=1), np.concatenate([q[1] for q in qs], axis=1))
def put(q, e, v):
    c, s = q[0].reshape(128, -1, 4).copy(), q[1].copy(); c[:, e] = v[0].reshape(128, -1, 4); s[:, e] = v[1]
    return (c.reshape(128, -1), s)
def pk(c, s):
    return (np.ascontiguousarray(c), mx_ref.live(s))
def emit(q):
    return q[0], q[1]
def packed(v, rng):
    q = [mx_ref.quantize(np.ascontiguousarray(v[r])) for r in range(N)]
    return np.stack([a for a, b in q]), np.stack([mx_ref.plane(b, rng) for a, b in q])
def values_of_codes():
    e, c = np.zeros((128, 128, 4), np.float32), np.zeros((128, 2, 4), np.uint8)
    e[np.arange(128), np.arange(128), 0] = 1
    c[:127, :, 0] = np.arange(256).reshape(2, 128).T[:127]
    return mx_ref.matmul(mx_ref.quantize(e.reshape(128, 512).astype(BF)), (c.reshape(128, 8), np.full((16, 2), 127, np.uint8))).T.reshape(-1).astype(np.float64)
CODE_VALUE, SCALE_VALUE = values_of_codes(), 2.0 ** (np.arange(256) - 127.0)
def decode(q):
    return (CODE_VALUE[q[0]].reshape(16, 8, -1, 4) * SCALE_VALUE[q[1]][:, None, :, None] + 0.0).reshape(128, -1).astype(np.float32)
def f(rng, *shape):
    return mx_ref.flush((rng.standard_normal(shape, dtype=np.float32) * np.exp2(rng.integers(-2, 3, shape[:-1] + (1,)))).astype(BF))
def wide(rng, *shape, cols=0):
    v = rng.standard_normal(shape, dtype=np.float32) * np.exp2(rng.integers(-12, 13, shape)).astype(np.float32)
    if cols: v *= np.repeat(np.exp2(rng.integers(-cols, cols + 1, shape[:-2] + (1, shape[-1] // 4))) * (rng.random(shape[:-2] + (1, shape[-1] // 4)) > 0.0625), 4, axis=-1).astype(np.float32)
    return mx_ref.flush(v.astype(BF))
C = 352
STEP = [1, 4, 2]
def at(t, e):
    return np.take_along_axis(t, e, axis=1)
def ext(e):
    return np.concatenate([e, np.full((len(e), 1), C)], axis=1)
def numbers_of(rng):
    return {"x": np.array(f(rng, N, 128, 4 * C)), "u": np.array(f(rng, N, 128, 512)), "v": np.array(f(rng, N, 128, 512))}
def trees(rng, kind, o=None):
    n, kind = 8 * N, kind.reshape(-1)
    t = np.arange(n)
    if o is None: o = rng.permuted(np.tile(np.arange(C), (n, 1)), axis=1)
    free = np.tile(np.arange(C + 1), (n, 1))
    e = np.full((3, n, C), C)
    for i in range(1, C):
        k = rng.integers(0, i + 1, n)
        side = np.where(kind == 1, rng.integers(0, 2, n), kind - 3)
        slot = np.where(kind == 0, free[t, k], np.where(kind == 2, i - 1, 2 * i - 2 + side))
        free[t, k] = 2 * i
        free[:, i + 1] = 2 * i + 1
        a = o[t, slot // 2]
        e[0, t, o[:, i]] = a
        e[1 + slot % 2, t, a] = o[:, i]
    return e.reshape(3, N, 8, C)
def depths(p):
    h = ext(p.reshape(8 * N, C))
    d = (h < C).astype(np.int64)
    for k in range(9):
        d = d + at(d, h)
        h = at(h, h)
    return d[:, :C].reshape(N, 8, C)
def stored(e):
    return {k: np.stack([gtable(e[i, r]) for r in range(N)]) for i, k in enumerate(("up", "lf", "rt"))}
def lists(rng):
    return stored(trees(rng, np.zeros((N, 8), np.int64)))
def mixed(rng):
    return np.stack([rng.permutation([0, 0, 0, 1, 1, 2, 3, 4]) for r in range(N)])
def layers(rng, still=[]):
    w = np.array(f(rng, N, 128, 2048)).reshape(N, 8, 16, 4, 8, 16, 4)
    for i in still:
        w[:, :, i] = 0
        w[:, :, :, :, :, i] = 0
    return w
def weights(rng, w):
    c, p = packed(np.ascontiguousarray(w).reshape(N, 128, 2048), rng)
    return {"wc": c, "ws": p}
def setup_inputs(rng):
    return {**numbers_of(rng), **lists(rng), **weights(rng, layers(rng))}
def setup_inputs_ties(rng):
    d = numbers_of(rng)
    o = rng.permutation(N) % 4
    kind = mixed(rng)
    kind[o == 3] = 1
    e = trees(rng, kind)
    h = depths(e[0])
    k = rng.integers(0, 4, (N, 8, C))
    k[o == 0] = 5
    k[o == 1] = h[o == 1]
    k[o == 3] = h[o == 3] % 3 == 1
    x = d["x"].reshape(N, 8, 16, C, 4)
    x[:, :, :3] = 0
    u = d["u"].reshape(N, 128, 128, 4)
    u[:, :, ::16] = 0
    for i in range(3):
        x[:, :, i, :, 0] = (k // 8 ** i % 8).astype(np.float32).astype(BF)
        for c in range(0, 128, 16): u[:, c + i, c, 0] = 8.0 ** i
    return {"x": x.reshape(N, 128, 4 * C), "u": u.reshape(N, 128, 512), "v": d["v"], **stored(e), **weights(rng, layers(rng, [0, 1, 2]))}
def setup_inputs_near(rng):
    d = numbers_of(rng)
    x = d["x"].astype(np.float32).reshape(N, 8, 16, C, 4)
    x[:, :, 0] = 0
    x[:, :, 8:] = 0
    u = d["u"].reshape(N, 128, 128, 4)
    u[:, :, ::16] = 0
    o = (np.arange(N) + rng.integers(4)) % 4
    for r in range(N):
        c = np.where(rng.permutation(8)[:, None] < 4, rng.choice([-1.0, 1.0], (8, 1)), rng.choice([-1.0, 1.0], (8, C)))
        s = rng.integers(0, 16, (8, C))
        digits = ((s[:, :, None] >> np.arange(4)) & 1) * np.exp2(np.arange(4) - 23.0)
        if o[r] < 2:
            x[r, :, 0, :, 0] = c
            x[r, :, 8] = digits
            x[r, :, 11, :, 0] = c * 2.0 ** -10
        elif o[r] == 2: x[r, :, 8] = digits * rng.choice([-1.0, 1.0], (8, C, 1))
        else:
            a = rng.choice([-1.0, 1.0], (8, 1)) * 2.0 ** -30
            x[r, :, 8, :, 0] = np.where(s < 8, 1.25, 0.0) * a
            x[r, :, 9, :, 0] = np.where(s < 8, 0.0, 1.125) * a
            for g in rng.permutation(8)[:4]:
                e = rng.choice([-1.0, 1.0], C) * 2.0 ** -30
                x[r, g, 8, :, 0] = 1.25 * e
                x[r, g, 9, :, 0] = -1.125 * e
        if o[r] > 1: x[r, :, 12, :, 0] = rng.choice([1.0, 1.5], (8, C)) * 2.0 ** -30
        place = [0, C - 1, int(rng.integers(C)), int(rng.integers(C))]
        for g, j in zip(rng.permutation(8)[:4], place): x[r, g, 0, j, 0] = 2.0 ** 29 * rng.choice([-1.0, 1.0])
        k = 1.0 if o[r] == 0 else 2.0 ** -30
        for h in range(0, 128, 16):
            u[r, h, h, 0] = k if o[r] < 2 else 1.0
            if o[r] < 2: u[r, h + 11, h, 0] = k
            if o[r] < 3: u[r, h + 8, h] = k
            else:
                u[r, h + 8, h, 0] = k
                u[r, h + 9, h, 0] = 1.125 * k
                u[r, h + 10, h, 0] = k
    w = layers(rng, [0, 8, 9, 10, 11, 12, 13, 14, 15])
    for g in range(8): w[:, g, 12, 0, g, 10, 0] = 2.0 ** -8
    return {"x": x.reshape(N, 128, 4 * C).astype(BF), "u": u.reshape(N, 128, 512), "v": d["v"], **stored(trees(rng, mixed(rng))), **weights(rng, w)}
def setup_inputs_odd(rng):
    d = numbers_of(rng)
    o = rng.permutation(N) % 2
    x = (1.0 + (2 * rng.integers(0, 64, (N, 16, 8, C, 4)) + 1) * 2.0 ** -7) * np.exp2(-rng.integers(0, 7, (N, 16, 8, C, 4)).astype(np.float64)) * rng.choice([-1.0, 1.0], (N, 16, 8, C, 4))
    x[:, :, 0, :, 0] = rng.choice([1.96875, 1.875], (N, 16, C)) * 2.0 ** 8 * rng.choice([-1.0, 1.0], (N, 16, 1))
    u = d["u"].reshape(N, 16, 8, 128, 4)
    u[:, :, 0, ::16] = 0
    for r in range(N):
        if o[r]: continue
        for g, i in enumerate(rng.permutation(8) % 2):
            x[r, 2 * g, 1, :, 0] = (8 + rng.integers(0, 2, C)) * 2.0 ** (i - 8.0)
            u[r, :, :, 16 * g] = 0
            u[r, 2 * g, 1, 16 * g, 0] = 1.0
    return {"x": x.astype(np.float32).reshape(N, 128, 4 * C).astype(BF), "u": u.reshape(N, 128, 512), "v": d["v"], **lists(rng), **weights(rng, layers(rng, [0, 8]))}
def setup_inputs_ends(rng):
    d = numbers_of(rng)
    o = (np.arange(N) + rng.integers(4)) % 4
    big = (o < 2)[:, None, None, None]
    def sized(*n):
        return np.where(big, (0.955 + 0.02 * rng.random((N,) + n)) * 2.0 ** 30, (1.0 + 0.125 * rng.integers(0, 8, (N,) + n)) * 2.0 ** -30)
    s = rng.choice([-1.0, 1.0], (N, 128, C, 4))
    s[o == 1] = rng.choice([-1.0, 1.0], (N, 1, C, 1))[o == 1]
    s[o == 3] = rng.choice([-1.0, 1.0], (N, 128, 1, 4))[o == 3]
    s[o % 2 == 0] = -1
    x = s * sized(128, C, 4)
    h = np.stack([rng.permutation(8) for r in range(N)])
    u = d["u"].reshape(N, 128, 128, 4)
    u[:, :, ::16] = (np.where(h < 2, 0.0, h % 2 * 2.0 - 1.0)[:, None, :, None] * sized(128, 8, 4)).astype(np.float32).astype(BF)
    v = rng.choice([-1.0, 1.0], (N, 128, 128, 4)) * sized(128, 128, 4)
    w = np.zeros((N, 128, 4, 128, 4), np.float32)
    i = np.arange(128)
    for b in range(4): w[:, i, b, i, b] = np.array([-0.125, -0.125, -2.0 ** -8, 2.0 ** 4])[o][:, None]
    kind = np.stack([rng.permutation([0, 1, 2, 2, 3, 3, 4, 4]) for r in range(N)])
    fall = np.stack([rng.permutation(8) % 2 for r in range(N)]).reshape(-1, 1)
    k = np.tile(np.arange(C), (8 * N, 1))
    return {"x": x.astype(np.float32).reshape(N, 128, 4 * C).astype(BF), "u": u.reshape(N, 128, 512), "v": v.astype(np.float32).reshape(N, 128, 512).astype(BF), **stored(trees(rng, kind, np.where(fall == 0, k, C - 1 - k))), **weights(rng, w.astype(BF))}
def setup_inputs_spread(rng):
    d = setup_inputs(rng)
    d["x"] = wide(rng, N, 128, 4 * C, cols=6)
    return d
def check_inputs(d):
    b = []
    for k in ("x", "u", "v"):
        a = np.abs(d[k].astype(np.float32))
        if not (np.isfinite(a).all() and ((a == 0) | (a >= 2.0 ** -30) & (a <= 2.0 ** 30)).all()): b.append("a value of " + k)
    bad = [k for k in ("up", "lf", "rt") if not ((d[k] >= 0) & (d[k] <= C)).all()]
    b += ["an entry of " + k for k in bad]
    none, least, most = [emit(mx_ref.quantize(np.full((128, 16), k, np.float32).astype(BF)))[1][0, 0] for k in (0.0, 2.0 ** -8, 2.0 ** 8)]
    own = np.arange(C + 1)
    for r in range(N):
        if ((d["wc"][r] == 0x7F) | (d["wc"][r] == 0xFF)).any(): b.append("wc: a code that is no number")
        s = mx_ref.live(d["ws"][r])
        if ((s != none) & ((s < least) | (s > most))).any(): b.append("ws: a scale out of range")
        if bad: continue
        p, l, e = [ext(gentries(d[k][r])) for k in ("up", "lf", "rt")]
        ok = (np.sum(p[:, :C] == C, axis=1) == 1).all() and (np.sum(l < C, axis=1) + np.sum(e < C, axis=1) == C - 1).all()
        ok = ok and ((l == C) | (l != e)).all() and all(((k == C) | (at(p, k) == own)).all() for k in (l, e))
        for k in range(9): p = at(p, p)
        if not (ok and (p == C).all()): b.append("up, lf, rt: not a tree")
    return b
def rotated(s, p, l, r):
    own = np.tile(np.arange(C + 1), (8, 1))
    w = np.concatenate([s, np.zeros((8, 1), np.float32)], axis=1)
    gain = np.where(p < C, np.maximum(w - at(w, p), np.float32(0)), np.float32(0))
    def better(a, b):
        i, j = at(gain, a), at(gain, b)
        return np.where((i > j) | (i == j) & (a < b), a, b)
    child = better(l, r)
    best = better(better(own, child), better(at(child, l), at(child, r)))
    z = at(p, p)
    g, v = np.nonzero((gain > 0) & (best == own) & (at(best, p) == own) & ((z == C) | (at(best, z) == own)))
    y, z = p[g, v], z[g, v]
    left, high = l[g, y] == v, l[g, z] == y
    c = np.where(left, r[g, v], l[g, v])
    a, b, e = p.copy(), l.copy(), r.copy()
    a[g, c], a[g, y], a[g, v] = y, v, z
    b[g, y], e[g, y] = np.where(left, c, l[g, y]), np.where(left, r[g, y], c)
    b[g, v], e[g, v] = np.where(left, l[g, v], y), np.where(left, y, r[g, v])
    b[g, z], e[g, z] = np.where(high, v, l[g, z]), np.where(high, r[g, z], v)
    for k in (a, b, e): k[:, C] = C
    return a, b, e
def reference(x, u, v, up, lf, rt, wc, ws):
    qu = [mx_ref.quantize(u[r]) for r in range(N)]
    lay = [pk(wc[r], ws[r]) for r in range(N)]
    link = [[ext(gentries(k[r])) for k in (up, lf, rt)] for r in range(N)]
    now = [x[r] for r in range(N)]
    for step in STEP:
        t, par, z = [], [], []
        for r in range(N):
            q = mx_ref.quantize(now[r])
            link[r] = rotated(mx_ref.matmul(qu[r], q)[::16] + np.float32(0.0), *link[r])
            p = link[r][0][:, :C]
            a = np.where(p == C, np.arange(C), p)
            t.append(decode(q))
            par.append(a)
            m = t[r].astype(BF)
            z.append(mx_ref.quantize(((gcols(m, a).astype(np.float32) + gcols(m, at(a, a)).astype(np.float32)) * np.float32(0.5)).astype(BF)))
        for r in range(N):
            now[r] = tile([gpick(mx_ref.matmul(pick(lay[r], np.arange(128 * b, 128 * b + 128)), z[(r - step) % N]) * np.float32(0.03125), par[r]) + t[r][:, b::4] for b in range(4)])
    y, tr = np.zeros((N, 128, C), np.float32), np.zeros((N, 8, 3 * C), np.float32)
    oc, osc = np.zeros((N, 128, 4 * C), np.uint8), np.zeros((N, 16, C), np.uint8)
    for r in range(N):
        q = mx_ref.quantize(now[r])
        y[r] = mx_ref.matmul(mx_ref.quantize(v[r]), q)
        tr[r] = np.concatenate([k[:, :C] for k in link[r]], axis=1)
        oc[r], osc[r] = emit(q)
    return {"y": y, "tr": tr, "oc": oc, "osc": osc}

from concourse.mybir import dt, AluOpType as OP, ActivationFunctionType as AF

C = 352
STEP = [1, 4, 2]
BIG = 1.0e29
BF, F32, I32, U16, U8, F8 = "bfloat16", "float32", "int32", "uint16", "uint8", "float8_e4m3fn_x4"
SCRATCH = {}
PART = {}


def _declare():
    def sb(names, n, d):
        for name in names.split():
            SCRATCH[name] = ("sbuf", [128, n], d)
    sb("xt fw fp fo pw zt xn", 1408, BF)
    sb("ut vt", 512, BF)
    sb("ones eb", 528, BF)
    sb("Bin BR Rin Ain LRin TA2 GT9", 352, BF)
    sb("G3 GT3 G5 GT5 G8 GT8", 704, BF)
    sb("G4 GT4", 1056, BF)
    sb("RR", 368, BF)
    sb("c32", 32, BF)
    sb("iot ST ST2 ST3", 384, BF)
    sb("AR LRR AAR", 400, BF)
    sb("rw", 1408, F32)
    sb("G", 1064, F32)
    sb("GT", 1056, F32)
    sb("G2 GT2", 704, F32)
    sb("r3 srow sown Hin trb yb", 352, F32)
    sb("HR", 360, F32)
    at = 0
    for names, n in (("NT3 E3 EN", 66), ("M2 OT2 D12 P1 w2 LM TLR DB rv rd v0 fy yk v1 nx dx gx gd", 44),
                     ("Mb OC m1 n1 m2 Bv n2 BN f1 f0 f01 e1 e2 r1 D3 rch u1 u2 u3 INN sR sR2 sL rc0 rc s0 s00 s1 AM w1 w3a w3b w3 isr cn ic", 22)):
        for name in names.split():
            PART[name] = (at, n)
            at += n
    sb("small", at, F32)
    sb("li pi k2 bi p31 pb", 44, I32)
    sb("ui oi p15 ow fu fd ai", 22, I32)
    sb("a0 a1 a2 a3 aa la1 la2 la3", 22, U16)
    sb("lr", 44, U16)
    for c, s, w in (("q1", "p1", C), ("q2", "p2", C), ("q3", "p3", C), ("q4", "p4", C), ("zq1", "zp1", C), ("zq2", "zp2", C),
                    ("zq3", "zp3", C), ("qz", "sz", C), ("qu", "su", 128), ("qv", "sv", 128), ("qe", "se", 512), ("wq", "wp", 512)):
        sb(c, w, F8)
        sb(s, w, U8)
    for i in range(8):
        SCRATCH["ps%d" % i] = ("psum", [128, 512], F32)


_declare()
SEMAPHORES = ["cv", "cs", "ct", "cg", "dx", "du", "dup", "dlr", "dw", "dv", "do1", "do2", "ls",
              "qa1", "qa2", "qa3", "lx1", "lx2", "lx3"]


def rank_program(g, core, T, topo):
    rank = T.rank_of(core)
    if rank is None:
        return
    sem = T.sem
    eng = {"v": g.vector, "s": g.scalar, "t": g.tensor, "g": g, "y": g.sync}
    csem = {"v": "cv", "s": "cs", "t": "ct", "g": "cg"}
    know = {q: {} for q in eng}
    total, snap, acc = {}, {}, {}

    def clash(a, b):
        (lo, hi, st), (l2, h2, s2) = a, b
        if st == s2 and st > 1 and (lo - l2) % st:
            return False
        return lo < h2 and l2 < hi

    def need(q, wants):
        w = {}
        for s, n in wants:
            if know[q].get(s, 0) < n:
                w[s] = max(w.get(s, 0), n)
        for s in sorted(w):
            if any(o != s and snap.get((o, w[o]), {}).get(s, 0) >= w[s] for o in w):
                continue
            eng[q].wait_ge(sem[s], w[s])
        for s in w:
            for k, n in list(snap.get((s, w[s]), {}).items()) + [(s, w[s])]:
                know[q][k] = max(know[q].get(k, 0), n)

    def hazards(q, reads, writes):
        out = []
        for vs, wr in ((reads, False), (writes, True)):
            for v in vs:
                psum = v[0][:2] == "ps"
                for (oq, s, n, ow, r) in acc.get(v[0], []):
                    if psum:
                        if not (oq == q and not ow and not wr):
                            out.append((s, n))
                    elif (wr or ow) and clash(r, v[1:]):
                        out.append((s, n))
        return out

    def record(q, s, n, reads, writes):
        for v in writes:
            old = acc.get(v[0], [])
            acc[v[0]] = [a for a in old if not (a[4][2] == v[3] and (a[4][0] - v[1]) % v[3] == 0 and a[4][0] >= v[1] and a[4][1] <= v[2])]
        for vs, wr in ((reads, False), (writes, True)):
            for v in vs:
                acc.setdefault(v[0], []).append((q, s, n, wr, tuple(v[1:])))

    def op(q, f, reads, writes):
        need(q, hazards(q, reads, writes))
        s = csem[q]
        n = total[s] = total.get(s, 0) + 1
        f().then_inc(sem[s], 1)
        snap[(s, n)] = dict(know[q])
        snap[(s, n)][s] = n
        record(q, s, n, reads, writes)

    def dma(q, s, out, src, reads=(), writes=()):
        need(q, hazards(q, reads, writes))
        n = total[s] = total.get(s, 0) + 16
        eng[q].dma_start(out, src).then_inc(sem[s], 16)
        snap[(s, n)] = dict(know[q])
        record("dma", s, n, reads, writes)

    def V(name, lo=0, hi=None, st=1):
        if name in PART:
            a, n = PART[name]
            return ("small", a + lo, a + (n if hi is None else hi), st)
        return (name, lo, SCRATCH[name][1][1] if hi is None else hi, st)

    def lane(name, i, k=0, n=1):
        return (name, C * k + i, C * (k + n), 16)

    def blk(name, i):
        return V(name, C * i, C * (i + 1))

    def SH(name, i):
        return V(name, 16 + i, 353 + i, 16)

    def ap(v):
        return T[v[0]][:, v[1]:v[2]] if v[3] == 1 else T[v[0]][:, v[1]:v[2]:v[3]]

    def ind(v, off):
        return ap(v).indirect(ap(off)) if off else ap(v)

    def tt(out, a, b, o, off=None):
        op("v", lambda: g.vector.tensor_tensor(ap(out), ind(a, off), ap(b), o), [a, b] + ([off] if off else []), [out])

    def ts(out, a, c1, o1, c2=None, o2=None):
        if o2 is None:
            op("v", lambda: g.vector.tensor_scalar(ap(out), ap(a), c1, None, o1), [a], [out])
        else:
            op("v", lambda: g.vector.tensor_scalar(ap(out), ap(a), c1, c2, o1, o2), [a], [out])

    def copy(out, a, off=None):
        op("v", lambda: g.vector.tensor_copy(ap(out), ind(a, off)), [a] + ([off] if off else []), [out])

    def act(out, a, off=None, scale=None, bias=None):
        def f():
            if bias is not None:
                return g.scalar.activation(ap(out), ind(a, off), AF.Identity, bias=bias, scale=scale)
            if scale is not None:
                return g.scalar.activation(ap(out), ind(a, off), AF.Copy, scale=scale)
            return g.scalar.activation(ap(out), ind(a, off), AF.Copy)
        op("s", f, [a] + ([off] if off else []), [out])

    def fill(v, c):
        op("v", lambda: g.vector.memset(ap(v), c), [], [v])

    def turn(out, a):
        op("v", lambda: g.vector.transpose(ap(out), ap(a)), [a], [out])

    def quant(c, s, a):
        op("v", lambda: g.vector.quantize_mx(ap(c), ap(s), ap(a)), [a], [c, s])

    def quant2(c, s, t):
        for i in (0, 176):
            quant(V(c, i, i + 176), V(s, i, i + 176), V(t, 4 * i, 4 * i + 704))

    def mx(bank, lc, ls, rc, rs):
        o = V("ps%d" % bank, 0, rc[2] - rc[1])
        op("t", lambda: g.tensor.matmul_mx(ap(o), ap(lc), ap(ls), ap(rc), ap(rs), True, True), [lc, ls, rc, rs], [o])
        return o

    def iota(v, pattern, base, cm, small=False):
        if small:
            op("g", lambda: g.iota(ap(v), pattern, base, cm, allow_small_or_imprecise_dtypes=True), [], [v])
        else:
            op("g", lambda: g.iota(ap(v), pattern, base, cm), [], [v])

    dma("y", "dx", ap(V("xt")), T.x[:, :], (), [V("xt")])
    dma("s", "dup", ap(V("ui")), T.up[:, :], (), [V("ui")])
    dma("s", "dlr", ap(V("li", 0, 22)), T.lf[:, :], (), [V("li", 0, 22)])
    dma("s", "dlr", ap(V("li", 22, 44)), T.rt[:, :], (), [V("li", 22, 44)])
    acc["li"] = [("dma", "dlr", 32, True, (0, 44, 1))]
    dma("s", "du", ap(V("ut")), T.u[:, :], (), [V("ut")])
    need("y", [("dx", 16)])
    dma("y", "dw", T.wq[:, 0:512].bitcast(dt.uint8), T.wc[:, :], (), [V("wq")])
    dma("y", "dw", ap(V("wp")), T.ws[:, :], (), [V("wp")])
    acc["wq"] = [("dma", "dw", 32, True, (0, 512, 1))]
    acc["wp"] = [("dma", "dw", 32, True, (0, 512, 1))]
    dma("y", "dv", ap(V("vt")), T.v[:, :], (), [V("vt")])

    fill(V("ones"), 1.0)
    iota(V("pi"), [[0, 44]], 0, 1)
    iota(V("oi"), [[16, 22]], -C, 0)
    iota(V("bi"), [[0, 2], [32, 11], [0, 2]], -176, 0)
    iota(V("k2"), [[0, 22], [1, 2]], 0, 0)
    iota(V("iot"), [[1, 384]], -176, 0, small=True)
    for n in ("Hin", "Ain", "Bin"):
        fill(V(n), 0.0)
    op("g", lambda: g.affine_select(ap(V("eb", 0, 520)), ap(V("ones", 0, 520)), [[-1, 520]], OP.is_equal, 0.0, 4, 4),
       [V("ones", 0, 520)], [V("eb", 0, 520)])
    ts(V("p15"), V("pi", 0, 22), 15, OP.bitwise_and)
    tt(V("ow"), V("p15"), V("oi"), OP.add)
    OT, M = V("OT2", 0, 22), V("M2", 0, 22)
    for n in ("AR", "AAR", "LRR"):
        fill(V(n, 0, 16), 0.0)
        if n != "AR":
            fill(V(n, 368, 400), 0.0)
    ts(V("p31"), V("pi"), 31, OP.bitwise_and)
    ts(V("pb"), V("pi"), 4, OP.arith_shift_right, 1, OP.bitwise_and)
    tt(V("OT2"), V("p31"), V("bi"), OP.add)
    tt(V("M2"), V("pb"), V("k2"), OP.is_equal)
    tt(V("Mb"), V("pb", 0, 22), V("k2", 0, 22), OP.not_equal)
    ts(V("OC"), OT, -1.0, OP.mult)
    ts(V("NT3", 44, 66), OT, -1.0, OP.mult, 176.0, OP.add)
    ts(V("cn"), OT, -1.0, OP.mult, 176.0, OP.add)
    fill(V("G", 1056, 1064), BIG)
    fill(V("HR", 352, 360), BIG)
    fill(V("RR", 352, 368), 0.0)
    fill(V("c32"), 0.0)
    ts(V("c32", 0, 32, 16), V("OT2", 0, 2), 0.0, OP.mult, 176.0, OP.add)
    turn(V("AR", 368, 400), V("c32"))
    ARw = V("AR", 16, 384)
    ARd, AAd, LRd = V("AR", 16, 368), V("AAR", 16, 368), V("LRR", 16, 368)
    LF, RT, AA = V("lr", 0, 22), V("lr", 22, 44), V("aa")
    A = [V("a%d" % i) for i in range(4)]
    TA, TAA, L, R, LR = lane("Ain", 0), lane("TA2", 0), V("TLR", 0, 22), V("TLR", 22, 44), V("TLR")

    ts(V("fu"), V("ui"), C, OP.is_equal)
    tt(V("fd"), V("fu"), V("ow"), OP.mult)
    tt(V("ai"), V("fd"), V("ui"), OP.add)
    copy(A[0], V("ai"))
    copy(V("lr"), V("li"))
    act(ARd, V("iot", 0, 368), A[0])
    act(blk("G8", 0), V("iot", 0, 368), LF)
    act(blk("G8", 1), V("iot", 0, 368), RT)
    act(AAd, ARw, A[0])
    for n in ("Rin", "LRin"):
        fill(V(n), 0.0)

    spare = []

    def later(*fs):
        spare.extend(fs)

    def gap(n=1):
        for i in range(min(n, len(spare))):
            spare.pop(0)()

    def kin():
        act(V("NT3", 0, 44), LR, scale=-1.0, bias=176.0)
        for n in ("Bin", "Rin"):
            act(lane(n, 2), L)
            act(lane(n, 3), R)

    def list_aa():
        later(
            lambda: turn(V("TA2"), AAd),
            lambda: turn(V("ST3"), V("AAR", 0, 384)),
            lambda: tt(V("w3a"), TAA, M, OP.mult),
            lambda: tt(V("w3b"), SH("ST3", 0), V("Mb"), OP.mult),
            lambda: tt(V("u3"), TAA, TA, OP.subtract),
            lambda: tt(V("w3"), V("w3a"), V("w3b"), OP.add),
            lambda: tt(V("u1"), OT, TAA, OP.subtract),
            lambda: ts(AA, V("w3"), 176.0, OP.add),
            lambda: tt(V("rch"), TAA, TA, OP.is_equal),
            lambda: tt(V("D12", 0, 22), L, TA, OP.subtract),
            lambda: tt(V("u2"), V("rch"), V("u1"), OP.mult),
            lambda: tt(V("D12", 22, 44), R, TA, OP.subtract),
            lambda: tt(V("D3"), V("u3"), V("u2"), OP.add))

    quant(V("qu"), V("su"), V("ut"))
    for b in range(4):
        quant(V("qe", 128 * b, 128 * b + 128), V("se", 128 * b, 128 * b + 128), V("eb", 4 - b, 516 - b))
    turn(V("GT9"), ARd)
    copy(TA, lane("GT9", 0))
    quant2("q1", "p1", "xt")
    later(lambda: turn(V("GT8"), V("G8")), lambda: copy(LR, lane("GT8", 0, 0, 2)), kin)
    list_aa()

    dst_of = [T.cores[(rank + d) % len(T.cores)] for d in STEP]

    def send(k, out_ap, in_ap, rsem):
        rid, pid = topo.addr(dst_of[k], core)
        g.remote_dma(out_ap, in_ap, sem[rsem], sem["ls"], pid, rid, topo.mask(core, dst_of[k]))
        total["ls"] = total.get("ls", 0) + len(topo.engines(core, dst_of[k]))

    def wait_read(q, v):
        need(q, hazards(q, [v], []))

    def arrived(k, names, s, calls):
        src = T.cores[(rank - STEP[k]) % len(T.cores)]
        n = calls * len(topo.engines(src, core))
        total[s] = n
        for m in names:
            acc[m] = [("far", s, n, True, (0, SCRATCH[m][1][1], 1))]

    for k in range(3):
        last = k == 2
        q, p = V("q%d" % (k + 1)), V("p%d" % (k + 1))
        S = [mx((0, 5, 6, 7)[i], V("qu"), V("su"), V(q[0], h, h + 176), V(p[0], h, h + 176)) for i, h in enumerate((0, 0, 176, 176))]
        Fb = [mx(1 + b, V("qe", 128 * b, 128 * b + 128), V("se", 128 * b, 128 * b + 128), q, p) for b in range(4)]
        zq, zp, la = "zq%d" % (k + 1), "zp%d" % (k + 1), "la%d" % (k + 1)
        wait_read("g", q)
        send(k, T[zq][:, 0:C].bitcast(dt.uint8), T[q[0]][:, 0:C].bitcast(dt.uint8), "qa%d" % (k + 1))
        send(k, T[zp][:, 0:C], T[p[0]][:, 0:C], "qa%d" % (k + 1))
        arrived(k, [zq, zp], "qa%d" % (k + 1), 2)
        arrived(k, [la], "lx%d" % (k + 1), 1)
        act(V("srow", 0, 176), S[0])
        act(V("srow", 176, 352), S[2])
        gap()
        copy(V("sown", 0, 176), S[1])
        copy(V("sown", 176, 352), S[3])
        gap()
        tt(blk("G", 2), V("srow"), V("sown"), OP.subtract, A[k])
        act(blk("G", 1), V("G", 704, 1064), RT)
        act(blk("G", 0), V("G", 704, 1064), LF)
        for b in range(2):
            act(blk("fo", b), Fb[b])
        turn(blk("GT", 2), blk("G", 2))
        gl, gr, ng = lane("GT", 0, 0), lane("GT", 0, 1), lane("GT", 0, 2)
        gap(3)
        ts(V("f1"), ng, 0.0, OP.is_lt)
        turn(blk("GT", 1), blk("G", 1))
        gap(2)
        tt(V("m1"), gr, ng, OP.min)
        turn(blk("GT", 0), blk("G", 0))
        gap()
        tt(lane("Hin", 0), V("m1"), gl, OP.min)
        gap()
        tt(V("E3", 22, 44), gr, lane("Hin", 0), OP.is_equal)
        tt(V("E3", 44, 66), ng, lane("Hin", 0), OP.is_equal)
        tt(V("E3", 0, 22), gl, lane("Hin", 0), OP.is_equal)
        gap()
        tt(V("EN"), V("E3"), V("NT3"), OP.mult)
        gap()
        tt(V("n1"), V("EN", 0, 22), V("EN", 22, 44), OP.max)
        gap()
        tt(lane("Hin", 1), V("n1"), V("EN", 44, 66), OP.max)
        gap()
        turn(V("HR", 0, 352), V("Hin"))
        act(blk("G2", 0), V("HR"), LF)
        gap()
        copy(blk("G2", 1), V("HR"), RT)
        act(blk("fo", 2), Fb[2])
        gap()
        turn(blk("GT2", 1), blk("G2", 1))
        hl, hr = lane("GT2", 0, 0), lane("GT2", 0, 1)
        gap()
        tt(V("m2"), hr, ng, OP.min)
        turn(blk("GT2", 0), blk("G2", 0))
        gap()
        tt(V("Bv"), V("m2"), hl, OP.min)
        gap()
        tt(V("E3", 22, 44), hr, V("Bv"), OP.is_equal)
        tt(V("E3", 44, 66), ng, V("Bv"), OP.is_equal)
        tt(V("E3", 0, 22), hl, V("Bv"), OP.is_equal)
        tt(V("EN", 44, 66), V("E3", 44, 66), V("NT3", 44, 66), OP.mult)
        tt(V("EN", 0, 44), V("E3", 0, 44), lane("GT2", 1, 0, 2), OP.mult)
        gap()
        tt(V("n2"), V("EN", 0, 22), V("EN", 22, 44), OP.max)
        gap()
        tt(V("BN"), V("n2"), V("EN", 44, 66), OP.max)
        gap()
        ts(lane("Bin", 0), V("BN"), -176.0, OP.add)
        gap()
        turn(V("BR"), V("Bin"))
        gap(len(spare))
        rot = lane("Rin", 0)
        act(blk("G3", 1), V("BR"), AA)
        copy(blk("G3", 0), V("BR"), A[k])
        tt(V("f0"), V("BN"), V("NT3", 44, 66), OP.is_equal)
        turn(blk("GT3", 0), blk("G3", 0))
        tt(V("f01"), V("f0"), V("f1"), OP.mult)
        tt(V("e1"), lane("GT3", 0, 0), V("OC"), OP.is_equal)
        turn(blk("GT3", 1), blk("G3", 1))
        tt(V("r1"), V("e1"), V("f01"), OP.mult)
        tt(V("e2"), lane("GT3", 0, 1), V("OC"), OP.is_equal)
        later(lambda: tt(V("sR"), lane("GT3", 3, 0), OT, OP.is_equal),
              lambda: tt(V("sR2"), lane("GT3", 3, 1), TA, OP.is_equal),
              lambda: tt(V("INN"), V("sR"), V("sR2"), OP.not_equal),
              lambda: ts(V("sL"), V("sR"), -1.0, OP.mult, 1.0, OP.add),
              lambda: tt(V("rv", 0, 22), V("sR"), rot, OP.mult),
              lambda: tt(V("rv", 22, 44), V("sL"), rot, OP.mult),
              lambda: tt(V("rd"), V("rv"), V("D12"), OP.mult),
              lambda: tt(V("v0"), LR, V("rd"), OP.subtract))
        gap()
        tt(rot, V("r1"), V("e2"), OP.mult)
        gap()
        turn(V("RR", 0, 352), V("Rin"))
        act(blk("G4", 0), V("RR"), LF)
        act(blk("G4", 1), V("RR"), RT)
        E = [(V("qe", 128 * b, 128 * b + 128), V("se", 128 * b, 128 * b + 128)) for b in range(4)]
        Fz = [mx((5, 6, 7, 1)[b], E[b][0], E[b][1], V(zq), V(zp)) for b in range(4)]
        for b in range(4):
            act(blk("fw", b), Fz[b], scale=0.5)
        gap()
        copy(blk("G4", 2), V("RR"), A[k])
        rl, rr = lane("GT4", 0, 0), lane("GT4", 0, 1)
        gap()
        turn(blk("GT4", 2), blk("G4", 2))
        gap()
        tt(V("rc0"), lane("GT4", 0, 2), V("INN"), OP.mult)
        gap()
        tt(V("rc"), V("rc0"), rot, OP.max)
        turn(blk("GT4", 0), blk("G4", 0))
        tt(V("s0"), V("rc"), V("D3"), OP.mult)
        tt(V("P1", 0, 22), rl, V("D12", 0, 22), OP.mult)
        tt(V("s00"), V("s0"), TA, OP.add)
        gap()
        tt(V("s1"), V("P1", 0, 22), V("s00"), OP.add)
        gap(len(spare))
        turn(blk("GT4", 1), blk("G4", 1))
        later(lambda: tt(V("DB", 0, 22), lane("GT4", 3, 0), L, OP.subtract),
              lambda: tt(V("DB", 22, 44), lane("GT4", 2, 1), R, OP.subtract),
              lambda: tt(V("fy"), lane("GT4", 0, 0, 2), V("rv"), OP.add),
              lambda: tt(V("yk"), lane("GT4", 0, 0, 2), V("DB"), OP.mult),
              lambda: tt(V("v1"), V("v0"), V("yk"), OP.add))
        tt(V("P1", 22, 44), rr, V("D12", 22, 44), OP.mult)
        gap()
        tt(TA, V("s1"), V("P1", 22, 44), OP.add)
        gap()
        tt(lane("Ain", 1), TA, V("Mb"), OP.mult)
        gap()
        turn(ARd, V("Ain"))
        tt(V("AM"), TA, M, OP.mult)
        turn(V("ST"), V("AR", 0, 384))
        gap()
        tt(V("w1"), V("AM"), SH("ST", 1), OP.add)
        gap()
        ts(A[k + 1], V("w1"), 176.0, OP.add)
        wait_read("g", A[k + 1])
        send(k, T[la][:, 0:22], ap(A[k + 1]), "lx%d" % (k + 1))
        act(blk("G5", 0), ARw, LF)
        act(blk("G5", 1), ARw, RT)
        for b in range(4):
            act(blk("fp", b), Fz[b], scale=0.5)
        if not last:
            act(AAd, ARw, A[k + 1])
        gap(len(spare))
        turn(V("GT5"), V("G5"))
        X2 = lane("GT5", 0, 0, 2)
        tt(V("nx"), X2, V("OT2"), OP.not_equal)
        tt(V("dx"), X2, LR, OP.subtract)
        tt(V("gx"), V("nx"), V("fy"), OP.subtract)
        tt(V("gd"), V("gx"), V("dx"), OP.mult)
        tt(LR, V("v1"), V("gd"), OP.add)
        if not last:
            later(lambda: tt(lane("LRin", 0), L, V("Mb"), OP.mult),
                  lambda: tt(lane("LRin", 1), R, V("Mb"), OP.mult),
                  lambda: tt(V("LM"), LR, V("M2"), OP.mult),
                  lambda: turn(LRd, V("LRin")),
                  lambda: turn(V("ST2"), V("LRR", 0, 384)),
                  lambda: tt(V("w2", 0, 22), V("LM", 0, 22), SH("ST2", 0), OP.add),
                  lambda: tt(V("w2", 22, 44), V("LM", 22, 44), SH("ST2", 1), OP.add),
                  lambda: ts(V("lr"), V("w2"), 176.0, OP.add))
            gap(5)
            list_aa()
        else:
            later(lambda: tt(V("isr"), TA, OT, OP.is_equal),
                  lambda: copy(lane("LRin", 0), L),
                  lambda: tt(V("ic"), V("isr"), V("cn"), OP.mult),
                  lambda: copy(lane("LRin", 1), R),
                  lambda: tt(lane("LRin", 2), TA, V("ic"), OP.add),
                  lambda: turn(LRd, V("LRin")))
        for b in range(4):
            tt(blk("pw", b), blk("fw", b), blk("fp", b), OP.add, V(la))
            if b < 3:
                act(V("zt", b, 1408, 4), blk("pw", b), V(la))
            else:
                act(V("zt", b, 768, 4), blk("pw", b), V(la, 0, 12))
        gap()
        copy(V("zt", 771, 1408, 4), blk("pw", 3), V(la, 12, 22))
        gap(2)
        quant2("qz", "sz", "zt")
        def layer(bank, b, lo, hi):
            return mx(bank, V("wq", 128 * b, 128 * b + 128), V("wp", 128 * b, 128 * b + 128), V("qz", lo, hi), V("sz", lo, hi))
        R0 = [layer(5, 0, 0, 176), layer(7, 0, 176, 352)]
        Rb = [layer((0, 6, 2, 3)[b], b, 0, 352) for b in range(1, 4)]
        act(V("rw", 0, 176), R0[0], scale=0.03125)
        for b in range(1, 4):
            act(blk("rw", b), Rb[b - 1], scale=0.03125)
        act(V("r3"), blk("rw", 3), A[k + 1])
        gap(3)
        ts(V("rw", 176, 352), R0[1], 0.03125, OP.mult)
        if last:
            quant(V("qv"), V("sv"), V("vt"))
        gap()
        for b in range(3):
            tt(V("xn", b, 1408, 4), blk("rw", b), blk("fo", b), OP.add, A[k + 1])
        tt(V("xn", 3, 1408, 4), V("r3"), Fb[3], OP.add)
        if not last:
            kin()
        else:
            act(V("trb"), LRd, scale=1.0, bias=176.0)
            for i, l in enumerate((2, 0, 1)):
                dma("y", "do1", T.tr[:, C * i:C * (i + 1)], T.trb[l:128:16, 0:C], [V("trb")])
        quant2("q%d" % (k + 2), "p%d" % (k + 2), "xn")

    q4, p4 = V("q4"), V("p4")
    ha = mx(0, V("qv"), V("sv"), V("q4", 0, 176), V("p4", 0, 176))
    hb = mx(6, V("qv"), V("sv"), V("q4", 176, 352), V("p4", 176, 352))
    dma("y", "do1", T.oc[:, :], T.q4[:, 0:C].bitcast(dt.uint8), [q4])
    copy(V("yb", 0, 176), ha)
    act(V("yb", 176, 352), hb)
    dma("s", "do2", T.y[:, 176:352], ap(V("yb", 176, 352)), [V("yb", 176, 352)])
    dma("y", "do1", T.y[:, 0:176], ap(V("yb", 0, 176)), [V("yb", 0, 176)])
    for i in range(4):
        dma("sy"[i % 2], ("do2", "do1")[i % 2], T.osc[4 * i:4 * i + 4, 0:C], T.p4[32 * i:32 * i + 4, 0:C], [p4])
    for s in sorted(total):
        if total[s] and know["g"].get(s, 0) < total[s]:
            g.wait_ge(sem[s], total[s])
